import numpy as np
import ml_dtypes


def mxq(x, axis, fmt="e4m3"):
    dtype, down = {"e4m3": (ml_dtypes.float8_e4m3fn, 7), "e5m2": (ml_dtypes.float8_e5m2, 14)}[fmt]
    v = np.moveaxis(np.asarray(x, np.float32).astype(ml_dtypes.bfloat16).astype(np.float64), axis, -1)
    blocks = v.reshape(v.shape[:-1] + (-1, 32))
    amax = np.abs(blocks).max(-1, keepdims=True)
    byte = np.maximum(np.where(amax > 0, np.frexp(amax)[1] - 1 + 127, 0) - down, 1)
    scale = np.exp2(byte - 127.0)
    codes = (blocks / scale).astype(np.float32).astype(dtype).astype(np.float64)
    return np.moveaxis((codes * scale).reshape(v.shape), -1, axis)


WIDE = False


def mx_kscale(k):
    if not WIDE:
        return np.ones(k)
    levels = np.array([10, -10, 5, -5, 0])
    if k % 512:
        return np.exp2(np.random.permutation(np.resize(levels, k // 32))).repeat(32)
    a = np.empty((k // 512, 16))
    for p in range(k // 512):
        a[p, :8] = np.random.permutation(np.resize(levels, 8))
        for g in range(8):
            far = levels[np.abs(levels - a[p, g]) >= 10]
            a[p, g + 8] = far[np.random.randint(len(far))]
    return np.exp2(a.ravel()).repeat(32)


def f64(x):
    return np.asarray(x).astype(np.float64)


def striped(idx):
    return np.tile(np.asarray(idx).reshape(-1, 16).T, (8, 1)).astype(np.uint16)


def unstriped(offs):
    return offs[:16].T.reshape(-1).astype(np.int64)


E2M1 = np.array([0.0, 0.5, 1.0, 1.5, 2.0, 3.0, 4.0, 6.0, -0.0, -0.5, -1.0, -1.5, -2.0, -3.0, -4.0, -6.0])


def pack_weight(w, fmt):
    k, n = w.shape
    w = f64(np.asarray(w, np.float32).astype(ml_dtypes.bfloat16)).reshape(k // 32, 32, n)
    amax = np.abs(w).max(1)
    if fmt == "e4m3":
        byte = np.frexp(amax)[1] - 1 + 127 - 7
    else:
        mant, ex = np.frexp(amax / 6.0)
        byte = np.where(mant > 0.5, ex, ex - 1) + 127
    byte = np.clip(np.where(amax > 0, byte, 1), 1, 254)
    scaled = (w * np.exp2(127.0 - byte)[:, None, :]).reshape(k, n).astype(np.float32)
    by_word = np.ascontiguousarray(scaled.reshape(k // 512, 128, 4, n).transpose(0, 1, 3, 2))
    if fmt == "e4m3":
        words = by_word.astype(ml_dtypes.float8_e4m3fn).view(np.uint8)
    else:
        c = by_word.astype(ml_dtypes.float4_e2m1fn).view(np.uint8) & 0xF
        words = (c[..., 0::2] | (c[..., 1::2] << 4)).reshape(k // 512, 128, 2 * n)
    return np.ascontiguousarray(words), np.ascontiguousarray(byte.astype(np.uint8).reshape(k // 512, 16, n))


def unpack_weight(words, scales, fmt):
    g, _, n = scales.shape
    words = np.ascontiguousarray(words).reshape(g, 128, n, -1)
    if fmt == "e4m3":
        vals = words.view(ml_dtypes.float8_e4m3fn).astype(np.float64)
    else:
        nib = np.empty((g, 128, n, 4), np.uint8)
        nib[..., 0::2] = words & 0xF
        nib[..., 1::2] = words >> 4
        vals = E2M1[nib]
    vals = vals * np.repeat(np.exp2(scales.astype(np.float64) - 127.0), 8, axis=1)[..., None]
    return vals.transpose(0, 1, 3, 2).reshape(g * 512, n)


def silu(v):
    return v / (1.0 + np.exp(-v))


def bf(x):
    return np.asarray(x, np.float32).astype(ml_dtypes.bfloat16)


def planes(Y):
    r, m = Y.shape
    b = f64(bf(Y)).reshape(r // 32, 32, m)
    amax = np.abs(b).max(1)
    byte = np.clip(np.where(amax > 0, np.frexp(amax)[1] - 1 + 127 - 7, 1), 1, 254)
    codes = (b * np.exp2(127.0 - byte)[:, None, :]).reshape(r, m).astype(np.float32).astype(ml_dtypes.float8_e4m3fn).view(np.uint8)
    words = codes.reshape(r // 512, 128, 4, m).transpose(0, 1, 3, 2)
    return np.ascontiguousarray(words), np.ascontiguousarray(byte.astype(np.uint8).reshape(r // 512, 16, m))


K, T, J, R, N = 1024, 1024, 512, 512, 512


def setup_inputs():
    n = np.random.standard_normal
    idx = np.random.permutation(T)[:J]
    fk = mx_kscale(K)
    fr = mx_kscale(R)
    xqp = pack_weight(n((K, T)) / fk[:, None], "e2m1")
    wsp = pack_weight(n((K, N)) * 1 / np.sqrt(K) * fk[:, None], "e2m1")
    wgp = pack_weight(n((K, R)) * 1 / np.sqrt(K) * fk[:, None], "e4m3")
    wdp = pack_weight(n((R, N)) * 1 / np.sqrt(R) / fr[:, None], "e2m1")
    return {
        "xq_words": xqp[0],
        "xq_scales": xqp[1],
        "ws_words": wsp[0],
        "ws_scales": wsp[1],
        "wg_words": wgp[0],
        "wg_scales": wgp[1],
        "wu": (n((K, R)) * 1 / np.sqrt(K) * fk[:, None] * fr).astype(np.float32),
        "wd_words": wdp[0],
        "wd_scales": wdp[1],
        "ga": (np.random.uniform(0.3, 1.0, (1, J))).astype(np.float32),
        "offs": striped(idx),
    }


def reference(xq_words, xq_scales, ws_words, ws_scales, wg_words, wg_scales, wu, wd_words, wd_scales, ga, offs):
    idx = unstriped(offs)
    xqu = unpack_weight(xq_words, xq_scales, "e2m1")
    wsu = unpack_weight(ws_words, ws_scales, "e2m1")
    wgu = unpack_weight(wg_words, wg_scales, "e4m3")
    wdu = unpack_weight(wd_words, wd_scales, "e2m1")
    s = wsu.T @ xqu
    xqidxg = xqu[:, idx]
    a = wgu.T @ xqidxg
    wuq = mxq(f64(wu), 0, "e4m3")
    b = wuq.T @ xqidxg
    hid = silu(a) * b
    hidq = mxq(hid, 0, "e4m3")
    p = wdu.T @ hidq
    pw = p * f64(ga)
    pg = np.zeros((N, T))
    pg[:, idx] = pw
    y = s + pg
    words, scales = planes(y)
    return y, words, scales

@@ -1,0 +1,279 @@
+from contextlib import ExitStack
+
+import concourse.mybir as mybir
+from concourse.masks import make_identity
+
+K, T, J, R, N = 1024, 1024, 512, 512, 512
+FLOPS = 2 * K * N * T + 2 * 2 * K * R * J + 2 * R * N * J
+
+F32 = mybir.dt.float32
+BF16 = mybir.dt.bfloat16
+I32 = mybir.dt.int32
+U32 = mybir.dt.uint32
+U16 = mybir.dt.uint16
+U8 = mybir.dt.uint8
+FP8X4 = mybir.dt.float8_e4m3fn_x4
+FP4X4 = mybir.dt.float4_e2m1fn_x4
+MULT = mybir.AluOpType.mult
+ADD = mybir.AluOpType.add
+SILU = mybir.ActivationFunctionType.Silu
+COPY = mybir.ActivationFunctionType.Copy
+
+P = 128
+PACK = 4
+PASSES = K // (P * PACK)
+BLOCKS = J // P
+HALF = T // 2
+WU_PIECES = [(0, slice(0, R)), (1, slice(0, R // 2)), (1, slice(R // 2, R))]
+
+
+def load_scale_rows(queue, plane, rows):
+    for quad in range(4):
+        queue.dma_start(
+            out=plane[32 * quad : 32 * quad + 4, :, :].bitcast(I32),
+            in_=rows[:, 4 * quad : 4 * quad + 4, :].rearrange("z r c -> r z c").bitcast(I32),
+        )
+
+
+def tile_list_expert_glu_shared_pl_kernel(
+    tc, xq_words, xq_scales, ws_words, ws_scales, wg_words, wg_scales, wu, wd_words, wd_scales, ga, offs,
+    out_0, out_1, out_2,
+):
+    nc = tc.nc
+    with ExitStack() as ctx:
+        keep = ctx.enter_context(tc.tile_pool(name="keep", bufs=1))
+        psum = ctx.enter_context(tc.psum_pool(name="psum", bufs=1))
+
+        def held(name, shape, dtype):
+            return keep.tile(shape, dtype, name=name, align_bytes=64)
+
+        def bank(name, shape, index):
+            return psum.tile(shape, F32, name=name, tag="bank%d" % index)
+
+        offsets = keep.tile([P, J // 16], U16, name="offsets")
+        x_words = [held("x_words%d" % z, [P, T], U16) for z in range(PASSES)]
+        x_scale = held("x_scale", [P, PASSES, T], U8)
+        wg_scale = held("wg_scale", [P, PASSES, R], U8)
+        wd_scale = held("wd_scale", [P, 1, N], U8)
+        ws_scale = held("ws_scale", [P, PASSES, N], U8)
+        wu_raw = [
+            keep.tile([P, PACK, cols.stop - cols.start], F32, name="wu_raw", tag="wu_raw%d" % i, align_bytes=64)
+            for i, (z, cols) in enumerate(WU_PIECES)
+        ]
+        wg_codes = held("wg_codes", [P, PASSES, R], U32)
+        wd_codes = held("wd_codes", [P, N], U16)
+        ws_codes = held("ws_codes", [P, PASSES, N], U16)
+        ga_col = held("ga_col", [P, BLOCKS], F32)
+        ident = held("ident", [P, P], F32)
+        zero = held("zero", [P, 1], F32)
+        silu_bias = held("silu_bias", [P, 1], F32)
+        pages = [held("page%d" % t, [P, T], F32) for t in range(PACK)]
+
+        nc.vector.memset(x_scale[:].bitcast(I32), 0)
+        nc.vector.memset(wg_scale[:].bitcast(I32), 0)
+        nc.vector.memset(zero[:], 0.0)
+        nc.vector.memset(wd_scale[:].bitcast(I32), 0)
+        nc.vector.memset(ws_scale[:].bitcast(I32), 0)
+
+        def load_wu(piece):
+            z, cols = WU_PIECES[piece]
+            rows = wu[z * P * PACK : (z + 1) * P * PACK, cols]
+            nc.sync.dma_start(out=wu_raw[piece][:], in_=rows.rearrange("(p t) c -> p t c", t=PACK))
+
+        nc.sync.dma_start(offsets[:], offs)
+        nc.sync.dma_start(out=x_words[0][:].bitcast(I32), in_=xq_words[0].bitcast(I32))
+        load_scale_rows(nc.sync, x_scale, xq_scales)
+        nc.sync.dma_start(out=x_words[1][:].bitcast(I32), in_=xq_words[1].bitcast(I32))
+        nc.sync.dma_start(
+            out=wg_codes[:].bitcast(I32), in_=wg_words.rearrange("z p n r -> p z (n r)").bitcast(I32)
+        )
+        load_scale_rows(nc.sync, wg_scale, wg_scales)
+        for piece in range(len(WU_PIECES)):
+            load_wu(piece)
+        nc.sync.dma_start(out=wd_codes[:].bitcast(I32), in_=wd_words[0].bitcast(I32))
+        nc.sync.dma_start(
+            out=ws_codes[:].bitcast(I32), in_=ws_words.rearrange("z p c -> p z c").bitcast(I32)
+        )
+        load_scale_rows(nc.sync, ws_scale, ws_scales)
+        with nc.allow_non_contiguous_dma(reason="one router weight to a partition"):
+            nc.sync.dma_start(out=ga_col[:], in_=ga.rearrange("o (c p) -> p (o c)", p=P))
+        load_scale_rows(nc.sync, wd_scale, wd_scales)
+
+        nc.scalar.activation(out=silu_bias[:], in_=zero[:], func=SILU)
+        make_identity(nc, ident[:])
+        for page in pages:
+            nc.gpsimd.memset(page[:], 0.0)
+
+        xg_words = [held("xg_words%d" % z, [P, J], U16) for z in range(PASSES)]
+        xg_scale = [held("xg_scale%d" % z, [P, J], U8) for z in range(PASSES)]
+        for z in range(PASSES):
+            nc.vector.tensor_copy(xg_words[z][:], x_words[z][:].indirect(offsets[:]))
+            nc.vector.tensor_copy(xg_scale[z][:], x_scale[:, z, :].indirect(offsets[:]))
+
+        def picked(z, jb):
+            cols = slice(jb * P, (jb + 1) * P)
+            return dict(lhsT=xg_words[z][:, cols].bitcast(FP4X4), lhsT_scale=xg_scale[z][:, cols])
+
+        wu_codes = [held("wu_codes%d" % z, [P, R], U32) for z in range(PASSES)]
+        wu_scale = [held("wu_scale%d" % z, [P, R], U8) for z in range(PASSES)]
+        for piece, (z, cols) in enumerate(WU_PIECES):
+            wu_bf = held("wu_bf%d" % piece, [P, cols.stop - cols.start, PACK], BF16)
+            copy = nc.scalar.copy if z == 0 else nc.vector.tensor_copy
+            copy(
+                out=wu_bf[:].rearrange("p (c i) t -> p c t i", i=4),
+                in_=wu_raw[piece][:].rearrange("p t (c i) -> p c t i", i=4),
+            )
+            nc.vector.quantize_mx(
+                out=wu_codes[z][:, cols].bitcast(FP8X4),
+                scales=wu_scale[z][:, cols],
+                in_=wu_bf[:].rearrange("p c t -> p (c t)"),
+            )
+
+        def by_word(ap):
+            return ap.rearrange("j (p u e) -> j u p e", u=2, e=2)
+
+        gate = keep.tile([P, BLOCKS, 2, P, 2], F32, name="gate", tag="wu_raw0", align_bytes=64)
+        for jb in range(BLOCKS):
+            a_ps = bank("a_ps", [P, R], 4 + jb)
+            for z in range(PASSES):
+                nc.tensor.matmul_mx(
+                    out=a_ps[:], rhs=wg_codes[:, z, :].bitcast(FP8X4), rhs_scale=wg_scale[:, z, :],
+                    start=(z == 0), stop=(z == PASSES - 1), **picked(z, jb),
+                )
+            nc.scalar.activation(out=gate[:, jb], in_=by_word(a_ps[:]), func=SILU, bias=silu_bias[:])
+
+        ups = [bank("b_ps", [P, R], jb) for jb in range(BLOCKS)]
+        for z in range(PASSES):
+            for jb in range(BLOCKS):
+                nc.tensor.matmul_mx(
+                    out=ups[jb][:], rhs=wu_codes[z][:].bitcast(FP8X4), rhs_scale=wu_scale[z][:],
+                    start=(z == 0), stop=(z == PASSES - 1), **picked(z, jb),
+                )
+
+        hid_grouped = []
+
+        def hidden(jb):
+            hid_t = held("hid_t%d" % jb, [P, 2, P, 2], BF16)
+            nc.vector.tensor_tensor(out=hid_t[:], in0=by_word(ups[jb][:]), in1=gate[:, jb], op=MULT)
+            words = hid_t[:].rearrange("j u p e -> j (u p e)").bitcast(F32)
+            turned = bank("turned", [P, 2, P], 4 + jb)
+            for u in range(2):
+                nc.tensor.transpose(turned[:, u, :], words[:, u * P : (u + 1) * P], ident[:])
+            grouped = held("hid_grouped%d" % jb, [P, P * PACK], BF16)
+            nc.scalar.copy(
+                out=grouped[:].bitcast(F32).rearrange("p (j u) -> p j u", u=2),
+                in_=turned[:].rearrange("p u j -> p j u"),
+            )
+            hid_grouped.append(grouped)
+
+        def down(jb):
+            codes = held("hid_codes%d" % jb, [P, P], U32)
+            scale = held("hid_scale%d" % jb, [P, P], U8)
+            nc.vector.quantize_mx(out=codes[:].bitcast(FP8X4), scales=scale[:], in_=hid_grouped[jb][:])
+            p_ps = bank("p_ps", [P, N], jb if jb < 2 else jb + 2)
+            nc.tensor.matmul_mx(
+                out=p_ps[:], lhsT=codes[:].bitcast(FP8X4), lhsT_scale=scale[:],
+                rhs=wd_codes[:].bitcast(FP4X4), rhs_scale=wd_scale[:, 0, :], start=True, stop=True,
+            )
+            pw_t = held("pw_t%d" % jb, [P, PACK, P], F32)
+            nc.scalar.activation(
+                out=pw_t[:], in_=p_ps[:].rearrange("j (m t) -> j t m", t=PACK),
+                func=COPY, scale=ga_col[:, jb : jb + 1],
+            )
+            back = bank("back", [P, PACK, P], 4 + jb)
+            for t in range(PACK):
+                nc.tensor.transpose(back[:, t, :], pw_t[:, t, :], ident[:])
+            nc.scalar.copy(out=pw[:, :, jb * P : (jb + 1) * P], in_=back[:])
+
+        pw = held("pw", [P, PACK, J], F32)
+        hidden(0)
+        hidden(1)
+        down(0)
+        down(1)
+        hidden(2)
+        hidden(3)
+        ws_dealt = held("ws_dealt", [P, PASSES, PACK, P], U16)
+        ws_scale_dealt = held("ws_scale_dealt", [P, PASSES, PACK, P], U8)
+        for z in range(PASSES):
+            nc.vector.tensor_copy(
+                out=ws_dealt[:, z, :, :], in_=ws_codes[:, z, :].rearrange("p (m t) -> p t m", t=PACK)
+            )
+            nc.vector.tensor_copy(
+                out=ws_scale_dealt[:, z, :, :], in_=ws_scale[:, z, :].rearrange("p (m t) -> p t m", t=PACK)
+            )
+
+        down(2)
+        down(3)
+
+
+        def scatter(t, lo, hi):
+            nc.vector.tensor_copy(pages[t][:].indirect(offsets[:, lo // 16 : hi // 16]), pw[:, t, lo:hi])
+
+        y = [[held("y%d_%d" % (u, h), [P, 2, HALF], F32) for h in range(2)] for u in range(2)]
+        y_bf = [held("y_bf%d" % h, [P, HALF, 2, 2], BF16) for h in range(2)]
+        out_rows = out_0.rearrange("(p t) c -> p t c", t=PACK)
+
+        def shared(t, h):
+            cols = slice(h * HALF, (h + 1) * HALF)
+            s_ps = bank("s_ps", [P, HALF], 6 + h)
+            for z in range(PASSES):
+                nc.tensor.matmul_mx(
+                    out=s_ps[:], lhsT=ws_dealt[:, z, t, :].bitcast(FP4X4), lhsT_scale=ws_scale_dealt[:, z, t, :],
+                    rhs=x_words[z][:, cols].bitcast(FP4X4), rhs_scale=x_scale[:, z, cols],
+                    start=(z == 0), stop=(z == PASSES - 1),
+                )
+            return s_ps
+
+        sums = {}
+        for t in range(PACK):
+            for h in range(2):
+                sums[t, h] = shared(t, h)
+                if t < 3:
+                    s_sb = held("s_sb%d_%d" % (t, h), [P, HALF], F32)
+                    nc.scalar.copy(out=s_sb[:], in_=sums[t, h][:])
+                    sums[t, h] = s_sb
+
+        def add_rows(t):
+            for h in range(2):
+                cols = slice(h * HALF, (h + 1) * HALF)
+                row = y[t // 2][h][:, t % 2, :]
+                engine = nc.gpsimd if t < 3 else nc.vector
+                engine.tensor_tensor(out=row, in0=sums[t, h][:], in1=pages[t][:, cols], op=ADD)
+                nc.sync.dma_start(out=out_rows[:, t, cols], in_=row)
+
+        def round_pair(copy, u, h):
+            copy(out=y_bf[h][:, :, u, :], in_=y[u][h][:].rearrange("p e c -> p c e"))
+
+        for jb in range(2):
+            scatter(0, jb * P, (jb + 1) * P)
+            scatter(1, jb * P, (jb + 1) * P)
+        scatter(0, J // 2, J)
+        scatter(1, J // 2, J)
+        scatter(2, 0, J)
+        scatter(3, 0, J)
+        add_rows(0)
+        add_rows(1)
+        add_rows(2)
+        for h in range(2):
+            round_pair(nc.scalar.copy, 0, h)
+        add_rows(3)
+        round_pair(nc.scalar.copy, 1, 0)
+        round_pair(nc.vector.tensor_copy, 1, 1)
+
+        y_scale = held("y_scale", [P, T], U8)
+        for h in (1, 0):
+            cols = slice(h * HALF, (h + 1) * HALF)
+            y_codes = held("y_codes%d" % h, [P, HALF], U32)
+            nc.vector.quantize_mx(
+                out=y_codes[:].bitcast(FP8X4), scales=y_scale[:, cols],
+                in_=y_bf[h][:].rearrange("p c u e -> p (c u e)"),
+            )
+            nc.sync.dma_start(
+                out=out_1[0].rearrange("p c r -> p (c r)").bitcast(I32)[:, cols], in_=y_codes[:].bitcast(I32)
+            )
+        for quad in range(4):
+            queue = nc.sync if quad % 2 else nc.scalar
+            queue.dma_start(
+                out=out_2[0, 4 * quad : 4 * quad + 4, :].bitcast(I32),
+                in_=y_scale[32 * quad : 32 * quad + 4, :].bitcast(I32),
+            )

@@ -17,22 +17,27 @@ FP4X4 = mybir.dt.float4_e2m1fn_x4
 MULT = mybir.AluOpType.mult
 ADD = mybir.AluOpType.add
 SILU = mybir.ActivationFunctionType.Silu
-COPY = mybir.ActivationFunctionType.Copy
 
 P = 128
 PACK = 4
 PASSES = K // (P * PACK)
 BLOCKS = J // P
-HALF = T // 2
-WU_PIECES = [(0, slice(0, R)), (1, slice(0, R // 2)), (1, slice(R // 2, R))]
+LIST_HALF = J // 2
+BANK = 512
+WU_PIECES = [(z, slice(c, c + R // 2)) for z in range(PASSES) for c in (0, R // 2)]
+S_BANKS = (0, 6, 0, 2)
 
 
-def load_scale_rows(queue, plane, rows):
+def load_scale_rows(nc, plane, rows):
     for quad in range(4):
-        queue.dma_start(
+        nc.sync.dma_start(
             out=plane[32 * quad : 32 * quad + 4, :, :].bitcast(I32),
             in_=rows[:, 4 * quad : 4 * quad + 4, :].rearrange("z r c -> r z c").bitcast(I32),
         )
+
+
+def deal(nc, dealt, plain):
+    nc.vector.tensor_copy(out=dealt, in_=plain.rearrange("p (m t) -> p t m", t=PACK))
 
 
 def tile_list_expert_glu_shared_pl_kernel(
@@ -44,8 +49,8 @@ def tile_list_expert_glu_shared_pl_kernel(
         keep = ctx.enter_context(tc.tile_pool(name="keep", bufs=1))
         psum = ctx.enter_context(tc.psum_pool(name="psum", bufs=1))
 
-        def held(name, shape, dtype):
-            return keep.tile(shape, dtype, name=name, align_bytes=64)
+        def held(name, shape, dtype, tag=""):
+            return keep.tile(shape, dtype, name=name, tag=tag or name, align_bytes=64)
 
         def bank(name, shape, index):
             return psum.tile(shape, F32, name=name, tag="bank%d" % index)
@@ -53,17 +58,14 @@ def tile_list_expert_glu_shared_pl_kernel(
         offsets = keep.tile([P, J // 16], U16, name="offsets")
         x_words = [held("x_words%d" % z, [P, T], U16) for z in range(PASSES)]
         x_scale = held("x_scale", [P, PASSES, T], U8)
-        wg_scale = held("wg_scale", [P, PASSES, R], U8)
-        wd_scale = held("wd_scale", [P, 1, N], U8)
-        ws_scale = held("ws_scale", [P, PASSES, N], U8)
-        wu_raw = [
-            keep.tile([P, PACK, cols.stop - cols.start], F32, name="wu_raw", tag="wu_raw%d" % i, align_bytes=64)
-            for i, (z, cols) in enumerate(WU_PIECES)
-        ]
         wg_codes = held("wg_codes", [P, PASSES, R], U32)
+        wg_scale = held("wg_scale", [P, PASSES, R], U8)
+        wu_raw = [held("wu_raw%d" % i, [P, PACK, R // 2], F32) for i in range(len(WU_PIECES))]
         wd_codes = held("wd_codes", [P, N], U16)
+        wd_scale = held("wd_scale", [P, 1, N], U8)
         ws_codes = held("ws_codes", [P, PASSES, N], U16)
-        ga_col = held("ga_col", [P, BLOCKS], F32)
+        ws_scale = held("ws_scale", [P, PASSES, N], U8)
+        ga_rows = held("ga_rows", [P, J], F32)
         ident = held("ident", [P, P], F32)
         zero = held("zero", [P, 1], F32)
         silu_bias = held("silu_bias", [P, 1], F32)
@@ -75,29 +77,20 @@ def tile_list_expert_glu_shared_pl_kernel(
         nc.vector.memset(wd_scale[:].bitcast(I32), 0)
         nc.vector.memset(ws_scale[:].bitcast(I32), 0)
 
-        def load_wu(piece):
-            z, cols = WU_PIECES[piece]
-            rows = wu[z * P * PACK : (z + 1) * P * PACK, cols]
-            nc.sync.dma_start(out=wu_raw[piece][:], in_=rows.rearrange("(p t) c -> p t c", t=PACK))
-
         nc.sync.dma_start(offsets[:], offs)
         nc.sync.dma_start(out=x_words[0][:].bitcast(I32), in_=xq_words[0].bitcast(I32))
-        load_scale_rows(nc.sync, x_scale, xq_scales)
+        load_scale_rows(nc, x_scale, xq_scales)
         nc.sync.dma_start(out=x_words[1][:].bitcast(I32), in_=xq_words[1].bitcast(I32))
-        nc.sync.dma_start(
-            out=wg_codes[:].bitcast(I32), in_=wg_words.rearrange("z p n r -> p z (n r)").bitcast(I32)
-        )
-        load_scale_rows(nc.sync, wg_scale, wg_scales)
-        for piece in range(len(WU_PIECES)):
-            load_wu(piece)
+        nc.sync.dma_start(out=wg_codes[:].bitcast(I32), in_=wg_words.rearrange("z p n r -> p z (n r)").bitcast(I32))
+        load_scale_rows(nc, wg_scale, wg_scales)
+        for raw, (z, cols) in zip(wu_raw, WU_PIECES):
+            rows = wu[z * P * PACK : (z + 1) * P * PACK, cols]
+            nc.sync.dma_start(out=raw[:], in_=rows.rearrange("(p t) c -> p t c", t=PACK))
         nc.sync.dma_start(out=wd_codes[:].bitcast(I32), in_=wd_words[0].bitcast(I32))
-        nc.sync.dma_start(
-            out=ws_codes[:].bitcast(I32), in_=ws_words.rearrange("z p c -> p z c").bitcast(I32)
-        )
-        load_scale_rows(nc.sync, ws_scale, ws_scales)
-        with nc.allow_non_contiguous_dma(reason="one router weight to a partition"):
-            nc.sync.dma_start(out=ga_col[:], in_=ga.rearrange("o (c p) -> p (o c)", p=P))
-        load_scale_rows(nc.sync, wd_scale, wd_scales)
+        load_scale_rows(nc, wd_scale, wd_scales)
+        nc.sync.dma_start(out=ga_rows[:], in_=ga[0].partition_broadcast(P))
+        nc.sync.dma_start(out=ws_codes[:].bitcast(I32), in_=ws_words.rearrange("z p c -> p z c").bitcast(I32))
+        load_scale_rows(nc, ws_scale, ws_scales)
 
         nc.scalar.activation(out=silu_bias[:], in_=zero[:], func=SILU)
         make_identity(nc, ident[:])
@@ -110,14 +103,14 @@ def tile_list_expert_glu_shared_pl_kernel(
             nc.vector.tensor_copy(xg_words[z][:], x_words[z][:].indirect(offsets[:]))
             nc.vector.tensor_copy(xg_scale[z][:], x_scale[:, z, :].indirect(offsets[:]))
 
-        def picked(z, jb):
+        def listed(z, jb):
             cols = slice(jb * P, (jb + 1) * P)
             return dict(lhsT=xg_words[z][:, cols].bitcast(FP4X4), lhsT_scale=xg_scale[z][:, cols])
 
         wu_codes = [held("wu_codes%d" % z, [P, R], U32) for z in range(PASSES)]
         wu_scale = [held("wu_scale%d" % z, [P, R], U8) for z in range(PASSES)]
         for piece, (z, cols) in enumerate(WU_PIECES):
-            wu_bf = held("wu_bf%d" % piece, [P, cols.stop - cols.start, PACK], BF16)
+            wu_bf = held("wu_bf%d" % piece, [P, R // 2, PACK], BF16)
             copy = nc.scalar.copy if z == 0 else nc.vector.tensor_copy
             copy(
                 out=wu_bf[:].rearrange("p (c i) t -> p c t i", i=4),
@@ -129,148 +122,145 @@ def tile_list_expert_glu_shared_pl_kernel(
                 in_=wu_bf[:].rearrange("p c t -> p (c t)"),
             )
 
-        def by_word(ap):
-            return ap.rearrange("j (p u e) -> j u p e", u=2, e=2)
+        def by_pair(row):
+            return row.rearrange("j (p u e) -> j u p e", u=2, e=2)
 
-        gate = keep.tile([P, BLOCKS, 2, P, 2], F32, name="gate", tag="wu_raw0", align_bytes=64)
+        gate = held("gate", [P, BLOCKS, 2, P, 2], F32, tag="wu_raw1")
         for jb in range(BLOCKS):
-            a_ps = bank("a_ps", [P, R], 4 + jb)
+            a_ps = bank("a_ps", [P, R], BLOCKS + jb)
             for z in range(PASSES):
                 nc.tensor.matmul_mx(
                     out=a_ps[:], rhs=wg_codes[:, z, :].bitcast(FP8X4), rhs_scale=wg_scale[:, z, :],
-                    start=(z == 0), stop=(z == PASSES - 1), **picked(z, jb),
+                    start=(z == 0), stop=(z == PASSES - 1), **listed(z, jb),
                 )
-            nc.scalar.activation(out=gate[:, jb], in_=by_word(a_ps[:]), func=SILU, bias=silu_bias[:])
+            nc.scalar.activation(out=gate[:, jb], in_=by_pair(a_ps[:]), func=SILU, bias=silu_bias[:])
 
-        ups = [bank("b_ps", [P, R], jb) for jb in range(BLOCKS)]
-        for z in range(PASSES):
-            for jb in range(BLOCKS):
+        b_ps = [bank("b_ps", [P, R], jb) for jb in range(BLOCKS)]
+        for jb in range(BLOCKS):
+            for z in range(PASSES):
                 nc.tensor.matmul_mx(
-                    out=ups[jb][:], rhs=wu_codes[z][:].bitcast(FP8X4), rhs_scale=wu_scale[z][:],
-                    start=(z == 0), stop=(z == PASSES - 1), **picked(z, jb),
+                    out=b_ps[jb][:], rhs=wu_codes[z][:].bitcast(FP8X4), rhs_scale=wu_scale[z][:],
+                    start=(z == 0), stop=(z == PASSES - 1), **listed(z, jb),
                 )
 
-        hid_grouped = []
+        wd_dealt = held("wd_dealt", [P, PACK, P], U16)
+        wd_scale_dealt = held("wd_scale_dealt", [P, PACK, P], U8)
+        deal(nc, wd_dealt[:], wd_codes[:])
+        deal(nc, wd_scale_dealt[:], wd_scale[:, 0, :])
 
-        def hidden(jb):
+        def hidden(jb, grouped):
             hid_t = held("hid_t%d" % jb, [P, 2, P, 2], BF16)
-            nc.vector.tensor_tensor(out=hid_t[:], in0=by_word(ups[jb][:]), in1=gate[:, jb], op=MULT)
+            nc.vector.tensor_tensor(out=hid_t[:], in0=by_pair(b_ps[jb][:]), in1=gate[:, jb], op=MULT)
             words = hid_t[:].rearrange("j u p e -> j (u p e)").bitcast(F32)
-            turned = bank("turned", [P, 2, P], 4 + jb)
+            turned = bank("turned", [P, 2, P], BLOCKS + jb)
             for u in range(2):
                 nc.tensor.transpose(turned[:, u, :], words[:, u * P : (u + 1) * P], ident[:])
-            grouped = held("hid_grouped%d" % jb, [P, P * PACK], BF16)
             nc.scalar.copy(
-                out=grouped[:].bitcast(F32).rearrange("p (j u) -> p j u", u=2),
+                out=grouped.bitcast(F32).rearrange("p (j u) -> p j u", u=2),
                 in_=turned[:].rearrange("p u j -> p j u"),
             )
-            hid_grouped.append(grouped)
 
-        def down(jb):
-            codes = held("hid_codes%d" % jb, [P, P], U32)
-            scale = held("hid_scale%d" % jb, [P, P], U8)
-            nc.vector.quantize_mx(out=codes[:].bitcast(FP8X4), scales=scale[:], in_=hid_grouped[jb][:])
-            p_ps = bank("p_ps", [P, N], jb if jb < 2 else jb + 2)
-            nc.tensor.matmul_mx(
-                out=p_ps[:], lhsT=codes[:].bitcast(FP8X4), lhsT_scale=scale[:],
-                rhs=wd_codes[:].bitcast(FP4X4), rhs_scale=wd_scale[:, 0, :], start=True, stop=True,
-            )
-            pw_t = held("pw_t%d" % jb, [P, PACK, P], F32)
-            nc.scalar.activation(
-                out=pw_t[:], in_=p_ps[:].rearrange("j (m t) -> j t m", t=PACK),
-                func=COPY, scale=ga_col[:, jb : jb + 1],
-            )
-            back = bank("back", [P, PACK, P], 4 + jb)
-            for t in range(PACK):
-                nc.tensor.transpose(back[:, t, :], pw_t[:, t, :], ident[:])
-            nc.scalar.copy(out=pw[:, :, jb * P : (jb + 1) * P], in_=back[:])
+        p_plain = [held("p_plain%d" % g, [P, 2, LIST_HALF], F32) for g in range(2)]
+        pw = held("pw", [P, 2, J], F32)
 
-        pw = held("pw", [P, PACK, J], F32)
-        hidden(0)
-        hidden(1)
-        down(0)
-        down(1)
-        hidden(2)
-        hidden(3)
+        def expert_half(g):
+            entries = slice(g * LIST_HALF, (g + 1) * LIST_HALF)
+            grouped = held("hid_grouped%d" % g, [P, 2, P * PACK], BF16)
+            for i in range(2):
+                hidden(2 * g + i, grouped[:, i, :])
+            codes = held("hid_codes%d" % g, [P, LIST_HALF], U32)
+            scale = held("hid_scale%d" % g, [P, LIST_HALF], U8)
+            nc.vector.quantize_mx(
+                out=codes[:].bitcast(FP8X4), scales=scale[:], in_=grouped[:].rearrange("p i c -> p (i c)")
+            )
+            for u in range(2):
+                p_ps = bank("p_ps", [P, 2, LIST_HALF], 2 * g + u)
+                for e in range(2):
+                    nc.tensor.matmul_mx(
+                        out=p_ps[:, e, :], lhsT=wd_dealt[:, 2 * u + e, :].bitcast(FP4X4),
+                        lhsT_scale=wd_scale_dealt[:, 2 * u + e, :],
+                        rhs=codes[:].bitcast(FP8X4), rhs_scale=scale[:], start=True, stop=True,
+                    )
+                if u == 0:
+                    nc.scalar.copy(out=p_plain[g][:], in_=p_ps[:])
+                else:
+                    for e in range(2):
+                        nc.vector.tensor_tensor(
+                            out=pw[:, e, entries], in0=p_ps[:, e, :], in1=ga_rows[:, entries], op=MULT
+                        )
+
+        for g in range(2):
+            expert_half(g)
+
         ws_dealt = held("ws_dealt", [P, PASSES, PACK, P], U16)
         ws_scale_dealt = held("ws_scale_dealt", [P, PASSES, PACK, P], U8)
         for z in range(PASSES):
-            nc.vector.tensor_copy(
-                out=ws_dealt[:, z, :, :], in_=ws_codes[:, z, :].rearrange("p (m t) -> p t m", t=PACK)
-            )
-            nc.vector.tensor_copy(
-                out=ws_scale_dealt[:, z, :, :], in_=ws_scale[:, z, :].rearrange("p (m t) -> p t m", t=PACK)
-            )
+            deal(nc, ws_dealt[:, z], ws_codes[:, z, :])
+            deal(nc, ws_scale_dealt[:, z], ws_scale[:, z, :])
 
-        down(2)
-        down(3)
-
-
-        def scatter(t, lo, hi):
-            nc.vector.tensor_copy(pages[t][:].indirect(offsets[:, lo // 16 : hi // 16]), pw[:, t, lo:hi])
-
-        y = [[held("y%d_%d" % (u, h), [P, 2, HALF], F32) for h in range(2)] for u in range(2)]
-        y_bf = [held("y_bf%d" % h, [P, HALF, 2, 2], BF16) for h in range(2)]
-        out_rows = out_0.rearrange("(p t) c -> p t c", t=PACK)
-
-        def shared(t, h):
-            cols = slice(h * HALF, (h + 1) * HALF)
-            s_ps = bank("s_ps", [P, HALF], 6 + h)
-            for z in range(PASSES):
-                nc.tensor.matmul_mx(
-                    out=s_ps[:], lhsT=ws_dealt[:, z, t, :].bitcast(FP4X4), lhsT_scale=ws_scale_dealt[:, z, t, :],
-                    rhs=x_words[z][:, cols].bitcast(FP4X4), rhs_scale=x_scale[:, z, cols],
-                    start=(z == 0), stop=(z == PASSES - 1),
-                )
-            return s_ps
-
-        sums = {}
+        shared = {}
         for t in range(PACK):
             for h in range(2):
-                sums[t, h] = shared(t, h)
-                if t < 3:
-                    s_sb = held("s_sb%d_%d" % (t, h), [P, HALF], F32)
-                    nc.scalar.copy(out=s_sb[:], in_=sums[t, h][:])
-                    sums[t, h] = s_sb
+                cols = slice(h * BANK, (h + 1) * BANK)
+                s_ps = bank("s_ps", [P, BANK], S_BANKS[t] + h)
+                for z in range(PASSES):
+                    nc.tensor.matmul_mx(
+                        out=s_ps[:], lhsT=ws_dealt[:, z, t, :].bitcast(FP4X4), lhsT_scale=ws_scale_dealt[:, z, t, :],
+                        rhs=x_words[z][:, cols].bitcast(FP4X4), rhs_scale=x_scale[:, z, cols],
+                        start=(z == 0), stop=(z == PASSES - 1),
+                    )
+                shared[t, h] = s_ps
+                if t < PACK - 1:
+                    shared[t, h] = held("s_sb%d_%d" % (t, h), [P, BANK], F32)
+                    nc.scalar.copy(out=shared[t, h][:], in_=s_ps[:])
 
-        def add_rows(t):
-            for h in range(2):
-                cols = slice(h * HALF, (h + 1) * HALF)
-                row = y[t // 2][h][:, t % 2, :]
-                engine = nc.gpsimd if t < 3 else nc.vector
-                engine.tensor_tensor(out=row, in0=sums[t, h][:], in1=pages[t][:, cols], op=ADD)
-                nc.sync.dma_start(out=out_rows[:, t, cols], in_=row)
+        for g in range(2):
+            entries = slice(g * LIST_HALF, (g + 1) * LIST_HALF)
+            half_list = offsets[:, g * LIST_HALF // 16 : (g + 1) * LIST_HALF // 16]
+            for t in range(2):
+                nc.vector.tensor_tensor(
+                    pages[t][:].indirect(half_list), p_plain[g][:, t, :], ga_rows[:, entries], MULT
+                )
+        for t in range(2, PACK):
+            nc.vector.tensor_copy(pages[t][:].indirect(offsets[:]), pw[:, t - 2, :])
+
+        y = [[held("y%d_%d" % (u, h), [P, 2, BANK], F32) for h in range(2)] for u in range(2)]
+        out_rows = out_0.rearrange("(p t) c -> p t c", t=PACK)
+
+        def add_page(engine, t, h):
+            cols = slice(h * BANK, (h + 1) * BANK)
+            row = y[t // 2][h][:, t % 2, :]
+            engine.tensor_tensor(out=row, in0=shared[t, h][:], in1=pages[t][:, cols], op=ADD)
+            nc.sync.dma_start(out=out_rows[:, t, cols], in_=row)
+
+        y_bf = [
+            held("y_bf%d" % h, [P, BANK, 2, 2], BF16, tag=tag) for h, tag in enumerate(("ws_dealt", "ws_scale_dealt"))
+        ]
 
         def round_pair(copy, u, h):
             copy(out=y_bf[h][:, :, u, :], in_=y[u][h][:].rearrange("p e c -> p c e"))
 
-        for jb in range(2):
-            scatter(0, jb * P, (jb + 1) * P)
-            scatter(1, jb * P, (jb + 1) * P)
-        scatter(0, J // 2, J)
-        scatter(1, J // 2, J)
-        scatter(2, 0, J)
-        scatter(3, 0, J)
-        add_rows(0)
-        add_rows(1)
-        add_rows(2)
         for h in range(2):
+            for t in range(2):
+                add_page(nc.gpsimd, t, h)
             round_pair(nc.scalar.copy, 0, h)
-        add_rows(3)
+        for h in range(2):
+            add_page(nc.gpsimd, 2, h)
+        for h in range(2):
+            add_page(nc.vector, PACK - 1, h)
         round_pair(nc.scalar.copy, 1, 0)
         round_pair(nc.vector.tensor_copy, 1, 1)
 
         y_scale = held("y_scale", [P, T], U8)
+        out_words = out_1[0].rearrange("p c r -> p (c r)").bitcast(I32)
         for h in (1, 0):
-            cols = slice(h * HALF, (h + 1) * HALF)
-            y_codes = held("y_codes%d" % h, [P, HALF], U32)
+            cols = slice(h * BANK, (h + 1) * BANK)
+            y_codes = held("y_codes%d" % h, [P, BANK], U32)
             nc.vector.quantize_mx(
                 out=y_codes[:].bitcast(FP8X4), scales=y_scale[:, cols],
                 in_=y_bf[h][:].rearrange("p c u e -> p (c u e)"),
             )
-            nc.sync.dma_start(
-                out=out_1[0].rearrange("p c r -> p (c r)").bitcast(I32)[:, cols], in_=y_codes[:].bitcast(I32)
-            )
+            nc.sync.dma_start(out=out_words[:, cols], in_=y_codes[:].bitcast(I32))
         for quad in range(4):
             queue = nc.sync if quad % 2 else nc.scalar
             queue.dma_start(

@@ -17,6 +17,7 @@ FP4X4 = mybir.dt.float4_e2m1fn_x4
 MULT = mybir.AluOpType.mult
 ADD = mybir.AluOpType.add
 SILU = mybir.ActivationFunctionType.Silu
+COPY = mybir.ActivationFunctionType.Copy
 
 P = 128
 PACK = 4
@@ -25,7 +26,7 @@ BLOCKS = J // P
 LIST_HALF = J // 2
 BANK = 512
 WU_PIECES = [(z, slice(c, c + R // 2)) for z in range(PASSES) for c in (0, R // 2)]
-S_BANKS = (0, 6, 0, 2)
+S_BANKS = (3, 5)
 
 
 def load_scale_rows(nc, plane, rows):
@@ -66,16 +67,15 @@ def tile_list_expert_glu_shared_pl_kernel(
         ws_codes = held("ws_codes", [P, PASSES, N], U16)
         ws_scale = held("ws_scale", [P, PASSES, N], U8)
         ga_rows = held("ga_rows", [P, J], F32)
+        ga_cols = held("ga_cols", [P, BLOCKS], F32)
         ident = held("ident", [P, P], F32)
         zero = held("zero", [P, 1], F32)
         silu_bias = held("silu_bias", [P, 1], F32)
         pages = [held("page%d" % t, [P, T], F32) for t in range(PACK)]
 
-        nc.vector.memset(x_scale[:].bitcast(I32), 0)
-        nc.vector.memset(wg_scale[:].bitcast(I32), 0)
-        nc.vector.memset(zero[:], 0.0)
-        nc.vector.memset(wd_scale[:].bitcast(I32), 0)
-        nc.vector.memset(ws_scale[:].bitcast(I32), 0)
+        nc.gpsimd.memset(zero[:], 0.0)
+        for plane in (x_scale, wg_scale, wd_scale, ws_scale):
+            nc.gpsimd.memset(plane[:].bitcast(I32), 0)
 
         nc.sync.dma_start(offsets[:], offs)
         nc.sync.dma_start(out=x_words[0][:].bitcast(I32), in_=xq_words[0].bitcast(I32))
@@ -91,6 +91,8 @@ def tile_list_expert_glu_shared_pl_kernel(
         nc.sync.dma_start(out=ga_rows[:], in_=ga[0].partition_broadcast(P))
         nc.sync.dma_start(out=ws_codes[:].bitcast(I32), in_=ws_words.rearrange("z p c -> p z c").bitcast(I32))
         load_scale_rows(nc, ws_scale, ws_scales)
+        with nc.allow_non_contiguous_dma(reason="one router weight to a partition"):
+            nc.sync.dma_start(out=ga_cols[:], in_=ga.rearrange("o (c p) -> p (o c)", p=P))
 
         nc.scalar.activation(out=silu_bias[:], in_=zero[:], func=SILU)
         make_identity(nc, ident[:])
@@ -160,37 +162,51 @@ def tile_list_expert_glu_shared_pl_kernel(
                 in_=turned[:].rearrange("p u j -> p j u"),
             )
 
+        hid_grouped = [held("hid_grouped%d" % g, [P, 2, P * PACK], BF16) for g in range(2)]
+        for jb in range(BLOCKS):
+            hidden(jb, hid_grouped[jb // 2][:, jb % 2, :])
+
         p_plain = [held("p_plain%d" % g, [P, 2, LIST_HALF], F32) for g in range(2)]
         pw = held("pw", [P, 2, J], F32)
-
-        def expert_half(g):
-            entries = slice(g * LIST_HALF, (g + 1) * LIST_HALF)
-            grouped = held("hid_grouped%d" % g, [P, 2, P * PACK], BF16)
-            for i in range(2):
-                hidden(2 * g + i, grouped[:, i, :])
-            codes = held("hid_codes%d" % g, [P, LIST_HALF], U32)
-            scale = held("hid_scale%d" % g, [P, LIST_HALF], U8)
-            nc.vector.quantize_mx(
-                out=codes[:].bitcast(FP8X4), scales=scale[:], in_=grouped[:].rearrange("p i c -> p (i c)")
-            )
-            for u in range(2):
-                p_ps = bank("p_ps", [P, 2, LIST_HALF], 2 * g + u)
-                for e in range(2):
-                    nc.tensor.matmul_mx(
-                        out=p_ps[:, e, :], lhsT=wd_dealt[:, 2 * u + e, :].bitcast(FP4X4),
-                        lhsT_scale=wd_scale_dealt[:, 2 * u + e, :],
-                        rhs=codes[:].bitcast(FP8X4), rhs_scale=scale[:], start=True, stop=True,
-                    )
-                if u == 0:
-                    nc.scalar.copy(out=p_plain[g][:], in_=p_ps[:])
-                else:
-                    for e in range(2):
-                        nc.vector.tensor_tensor(
-                            out=pw[:, e, entries], in0=p_ps[:, e, :], in1=ga_rows[:, entries], op=MULT
-                        )
-
+        hid_codes = [held("hid_codes%d" % g, [P, LIST_HALF], U32) for g in range(2)]
+        hid_scale = [held("hid_scale%d" % g, [P, LIST_HALF], U8) for g in range(2)]
         for g in range(2):
-            expert_half(g)
+            nc.vector.quantize_mx(
+                out=hid_codes[g][:].bitcast(FP8X4), scales=hid_scale[g][:],
+                in_=hid_grouped[g][:].rearrange("p i c -> p (i c)"),
+            )
+            p_ps = bank("p_ps", [P, 2, LIST_HALF], 2 * g)
+            for t in range(2):
+                nc.tensor.matmul_mx(
+                    out=p_ps[:, t, :], lhsT=wd_dealt[:, t, :].bitcast(FP4X4), lhsT_scale=wd_scale_dealt[:, t, :],
+                    rhs=hid_codes[g][:].bitcast(FP8X4), rhs_scale=hid_scale[g][:], start=True, stop=True,
+                )
+            nc.scalar.copy(out=p_plain[g][:], in_=p_ps[:])
+
+        wd_late = wd_dealt[:, 2:, :].rearrange("p t m -> p (t m)")
+        wd_scale_late = wd_scale_dealt[:, 2:, :].rearrange("p t m -> p (t m)")
+        for g in range(2):
+            pt_ps = bank("pt_ps", [P, 2, 2 * P], 2 * g + 1)
+            pw_t = held("pw_t%d" % g, [P, 2, 2, P], F32)
+            for i in range(2):
+                cols = slice(i * P, (i + 1) * P)
+                nc.tensor.matmul_mx(
+                    out=pt_ps[:, i, :], lhsT=hid_codes[g][:, cols].bitcast(FP8X4), lhsT_scale=hid_scale[g][:, cols],
+                    rhs=wd_late.bitcast(FP4X4), rhs_scale=wd_scale_late, start=True, stop=True,
+                )
+            for i in range(2):
+                jb = 2 * g + i
+                nc.scalar.activation(
+                    out=pw_t[:, i].rearrange("j e m -> j (e m)"), in_=pt_ps[:, i, :],
+                    func=COPY, scale=ga_cols[:, jb : jb + 1],
+                )
+            back = bank("back", [P, 2, 2, P], BLOCKS + g)
+            for e in range(2):
+                for i in range(2):
+                    nc.tensor.transpose(back[:, e, i, :], pw_t[:, i, e, :], ident[:])
+            nc.scalar.copy(
+                out=pw[:, :, g * LIST_HALF : (g + 1) * LIST_HALF], in_=back[:].rearrange("p e i j -> p e (i j)")
+            )
 
         ws_dealt = held("ws_dealt", [P, PASSES, PACK, P], U16)
         ws_scale_dealt = held("ws_scale_dealt", [P, PASSES, PACK, P], U8)
@@ -202,7 +218,7 @@ def tile_list_expert_glu_shared_pl_kernel(
         for t in range(PACK):
             for h in range(2):
                 cols = slice(h * BANK, (h + 1) * BANK)
-                s_ps = bank("s_ps", [P, BANK], S_BANKS[t] + h)
+                s_ps = bank("s_ps", [P, BANK], S_BANKS[h])
                 for z in range(PASSES):
                     nc.tensor.matmul_mx(
                         out=s_ps[:], lhsT=ws_dealt[:, z, t, :].bitcast(FP4X4), lhsT_scale=ws_scale_dealt[:, z, t, :],

from contextlib import ExitStack

import concourse.mybir as mybir
from concourse.masks import make_identity

K, T, J, R, N = 1024, 1024, 512, 512, 512
FLOPS = 2 * K * N * T + 2 * 2 * K * R * J + 2 * R * N * J

F32 = mybir.dt.float32
BF16 = mybir.dt.bfloat16
I32 = mybir.dt.int32
U32 = mybir.dt.uint32
U16 = mybir.dt.uint16
U8 = mybir.dt.uint8
FP8X4 = mybir.dt.float8_e4m3fn_x4
FP4X4 = mybir.dt.float4_e2m1fn_x4
MULT = mybir.AluOpType.mult
ADD = mybir.AluOpType.add
SILU = mybir.ActivationFunctionType.Silu
COPY = mybir.ActivationFunctionType.Copy

P = 128
PACK = 4
PASSES = K // (P * PACK)
BLOCKS = J // P
LIST_HALF = J // 2
BANK = 512
WU_PIECES = [(z, slice(c, c + R // 2)) for z in range(PASSES) for c in (0, R // 2)]
S_BANKS = (3, 5)


def load_scale_rows(nc, plane, rows):
    for quad in range(4):
        nc.sync.dma_start(
            out=plane[32 * quad : 32 * quad + 4, :, :].bitcast(I32),
            in_=rows[:, 4 * quad : 4 * quad + 4, :].rearrange("z r c -> r z c").bitcast(I32),
        )


def deal(nc, dealt, plain):
    nc.vector.tensor_copy(out=dealt, in_=plain.rearrange("p (m t) -> p t m", t=PACK))


def tile_list_expert_glu_shared_pl_kernel(
    tc, xq_words, xq_scales, ws_words, ws_scales, wg_words, wg_scales, wu, wd_words, wd_scales, ga, offs,
    out_0, out_1, out_2,
):
    nc = tc.nc
    with ExitStack() as ctx:
        keep = ctx.enter_context(tc.tile_pool(name="keep", bufs=1))
        psum = ctx.enter_context(tc.psum_pool(name="psum", bufs=1))

        def held(name, shape, dtype, tag=""):
            return keep.tile(shape, dtype, name=name, tag=tag or name, align_bytes=64)

        def bank(name, shape, index):
            return psum.tile(shape, F32, name=name, tag="bank%d" % index)

        offsets = keep.tile([P, J // 16], U16, name="offsets")
        x_words = [held("x_words%d" % z, [P, T], U16) for z in range(PASSES)]
        x_scale = held("x_scale", [P, PASSES, T], U8)
        wg_codes = held("wg_codes", [P, PASSES, R], U32)
        wg_scale = held("wg_scale", [P, PASSES, R], U8)
        wu_raw = [held("wu_raw%d" % i, [P, PACK, R // 2], F32) for i in range(len(WU_PIECES))]
        wd_codes = held("wd_codes", [P, N], U16)
        wd_scale = held("wd_scale", [P, 1, N], U8)
        ws_codes = held("ws_codes", [P, PASSES, N], U16)
        ws_scale = held("ws_scale", [P, PASSES, N], U8)
        ga_rows = held("ga_rows", [P, J], F32)
        ga_cols = held("ga_cols", [P, BLOCKS], F32)
        ident = held("ident", [P, P], F32)
        zero = held("zero", [P, 1], F32)
        silu_bias = held("silu_bias", [P, 1], F32)
        pages = [held("page%d" % t, [P, T], F32) for t in range(PACK)]

        nc.gpsimd.memset(zero[:], 0.0)
        for plane in (x_scale, wg_scale, wd_scale, ws_scale):
            nc.gpsimd.memset(plane[:].bitcast(I32), 0)

        nc.sync.dma_start(offsets[:], offs)
        nc.sync.dma_start(out=x_words[0][:].bitcast(I32), in_=xq_words[0].bitcast(I32))
        load_scale_rows(nc, x_scale, xq_scales)
        nc.sync.dma_start(out=x_words[1][:].bitcast(I32), in_=xq_words[1].bitcast(I32))
        nc.sync.dma_start(out=wg_codes[:].bitcast(I32), in_=wg_words.rearrange("z p n r -> p z (n r)").bitcast(I32))
        load_scale_rows(nc, wg_scale, wg_scales)
        for raw, (z, cols) in zip(wu_raw, WU_PIECES):
            rows = wu[z * P * PACK : (z + 1) * P * PACK, cols]
            nc.sync.dma_start(out=raw[:], in_=rows.rearrange("(p t) c -> p t c", t=PACK))
        nc.sync.dma_start(out=wd_codes[:].bitcast(I32), in_=wd_words[0].bitcast(I32))
        load_scale_rows(nc, wd_scale, wd_scales)
        nc.sync.dma_start(out=ga_rows[:], in_=ga[0].partition_broadcast(P))
        nc.sync.dma_start(out=ws_codes[:].bitcast(I32), in_=ws_words.rearrange("z p c -> p z c").bitcast(I32))
        load_scale_rows(nc, ws_scale, ws_scales)
        with nc.allow_non_contiguous_dma(reason="one router weight to a partition"):
            nc.sync.dma_start(out=ga_cols[:], in_=ga.rearrange("o (c p) -> p (o c)", p=P))

        nc.scalar.activation(out=silu_bias[:], in_=zero[:], func=SILU)
        make_identity(nc, ident[:])
        for page in pages:
            nc.gpsimd.memset(page[:], 0.0)

        xg_words = [held("xg_words%d" % z, [P, J], U16) for z in range(PASSES)]
        xg_scale = [held("xg_scale%d" % z, [P, J], U8) for z in range(PASSES)]
        for z in range(PASSES):
            nc.vector.tensor_copy(xg_words[z][:], x_words[z][:].indirect(offsets[:]))
            nc.vector.tensor_copy(xg_scale[z][:], x_scale[:, z, :].indirect(offsets[:]))

        def listed(z, jb):
            cols = slice(jb * P, (jb + 1) * P)
            return dict(lhsT=xg_words[z][:, cols].bitcast(FP4X4), lhsT_scale=xg_scale[z][:, cols])

        wu_codes = [held("wu_codes%d" % z, [P, R], U32) for z in range(PASSES)]
        wu_scale = [held("wu_scale%d" % z, [P, R], U8) for z in range(PASSES)]
        for piece, (z, cols) in enumerate(WU_PIECES):
            wu_bf = held("wu_bf%d" % piece, [P, R // 2, PACK], BF16)
            copy = nc.scalar.copy if z == 0 else nc.vector.tensor_copy
            copy(
                out=wu_bf[:].rearrange("p (c i) t -> p c t i", i=4),
                in_=wu_raw[piece][:].rearrange("p t (c i) -> p c t i", i=4),
            )
            nc.vector.quantize_mx(
                out=wu_codes[z][:, cols].bitcast(FP8X4),
                scales=wu_scale[z][:, cols],
                in_=wu_bf[:].rearrange("p c t -> p (c t)"),
            )

        def by_pair(row):
            return row.rearrange("j (p u e) -> j u p e", u=2, e=2)

        gate = held("gate", [P, BLOCKS, 2, P, 2], F32, tag="wu_raw1")
        for jb in range(BLOCKS):
            a_ps = bank("a_ps", [P, R], BLOCKS + jb)
            for z in range(PASSES):
                nc.tensor.matmul_mx(
                    out=a_ps[:], rhs=wg_codes[:, z, :].bitcast(FP8X4), rhs_scale=wg_scale[:, z, :],
                    start=(z == 0), stop=(z == PASSES - 1), **listed(z, jb),
                )
            nc.scalar.activation(out=gate[:, jb], in_=by_pair(a_ps[:]), func=SILU, bias=silu_bias[:])

        b_ps = [bank("b_ps", [P, R], jb) for jb in range(BLOCKS)]
        for jb in range(BLOCKS):
            for z in range(PASSES):
                nc.tensor.matmul_mx(
                    out=b_ps[jb][:], rhs=wu_codes[z][:].bitcast(FP8X4), rhs_scale=wu_scale[z][:],
                    start=(z == 0), stop=(z == PASSES - 1), **listed(z, jb),
                )

        wd_dealt = held("wd_dealt", [P, PACK, P], U16)
        wd_scale_dealt = held("wd_scale_dealt", [P, PACK, P], U8)
        deal(nc, wd_dealt[:], wd_codes[:])
        deal(nc, wd_scale_dealt[:], wd_scale[:, 0, :])

        def hidden(jb, grouped):
            hid_t = held("hid_t%d" % jb, [P, 2, P, 2], BF16)
            nc.vector.tensor_tensor(out=hid_t[:], in0=by_pair(b_ps[jb][:]), in1=gate[:, jb], op=MULT)
            words = hid_t[:].rearrange("j u p e -> j (u p e)").bitcast(F32)
            turned = bank("turned", [P, 2, P], BLOCKS + jb)
            for u in range(2):
                nc.tensor.transpose(turned[:, u, :], words[:, u * P : (u + 1) * P], ident[:])
            nc.scalar.copy(
                out=grouped.bitcast(F32).rearrange("p (j u) -> p j u", u=2),
                in_=turned[:].rearrange("p u j -> p j u"),
            )

        hid_grouped = [held("hid_grouped%d" % g, [P, 2, P * PACK], BF16) for g in range(2)]
        for jb in range(BLOCKS):
            hidden(jb, hid_grouped[jb // 2][:, jb % 2, :])

        p_plain = [held("p_plain%d" % g, [P, 2, LIST_HALF], F32) for g in range(2)]
        pw = held("pw", [P, 2, J], F32)
        hid_codes = [held("hid_codes%d" % g, [P, LIST_HALF], U32) for g in range(2)]
        hid_scale = [held("hid_scale%d" % g, [P, LIST_HALF], U8) for g in range(2)]
        for g in range(2):
            nc.vector.quantize_mx(
                out=hid_codes[g][:].bitcast(FP8X4), scales=hid_scale[g][:],
                in_=hid_grouped[g][:].rearrange("p i c -> p (i c)"),
            )
            p_ps = bank("p_ps", [P, 2, LIST_HALF], 2 * g)
            for t in range(2):
                nc.tensor.matmul_mx(
                    out=p_ps[:, t, :], lhsT=wd_dealt[:, t, :].bitcast(FP4X4), lhsT_scale=wd_scale_dealt[:, t, :],
                    rhs=hid_codes[g][:].bitcast(FP8X4), rhs_scale=hid_scale[g][:], start=True, stop=True,
                )
            nc.scalar.copy(out=p_plain[g][:], in_=p_ps[:])

        wd_late = wd_dealt[:, 2:, :].rearrange("p t m -> p (t m)")
        wd_scale_late = wd_scale_dealt[:, 2:, :].rearrange("p t m -> p (t m)")
        for g in range(2):
            pt_ps = bank("pt_ps", [P, 2, 2 * P], 2 * g + 1)
            pw_t = held("pw_t%d" % g, [P, 2, 2, P], F32)
            for i in range(2):
                cols = slice(i * P, (i + 1) * P)
                nc.tensor.matmul_mx(
                    out=pt_ps[:, i, :], lhsT=hid_codes[g][:, cols].bitcast(FP8X4), lhsT_scale=hid_scale[g][:, cols],
                    rhs=wd_late.bitcast(FP4X4), rhs_scale=wd_scale_late, start=True, stop=True,
                )
            for i in range(2):
                jb = 2 * g + i
                nc.scalar.activation(
                    out=pw_t[:, i].rearrange("j e m -> j (e m)"), in_=pt_ps[:, i, :],
                    func=COPY, scale=ga_cols[:, jb : jb + 1],
                )
            back = bank("back", [P, 2, 2, P], BLOCKS + g)
            for e in range(2):
                for i in range(2):
                    nc.tensor.transpose(back[:, e, i, :], pw_t[:, i, e, :], ident[:])
            nc.scalar.copy(
                out=pw[:, :, g * LIST_HALF : (g + 1) * LIST_HALF], in_=back[:].rearrange("p e i j -> p e (i j)")
            )

        ws_dealt = held("ws_dealt", [P, PASSES, PACK, P], U16)
        ws_scale_dealt = held("ws_scale_dealt", [P, PASSES, PACK, P], U8)
        for z in range(PASSES):
            deal(nc, ws_dealt[:, z], ws_codes[:, z, :])
            deal(nc, ws_scale_dealt[:, z], ws_scale[:, z, :])

        shared = {}
        for t in range(PACK):
            for h in range(2):
                cols = slice(h * BANK, (h + 1) * BANK)
                s_ps = bank("s_ps", [P, BANK], S_BANKS[h])
                for z in range(PASSES):
                    nc.tensor.matmul_mx(
                        out=s_ps[:], lhsT=ws_dealt[:, z, t, :].bitcast(FP4X4), lhsT_scale=ws_scale_dealt[:, z, t, :],
                        rhs=x_words[z][:, cols].bitcast(FP4X4), rhs_scale=x_scale[:, z, cols],
                        start=(z == 0), stop=(z == PASSES - 1),
                    )
                shared[t, h] = s_ps
                if t < PACK - 1:
                    shared[t, h] = held("s_sb%d_%d" % (t, h), [P, BANK], F32)
                    nc.scalar.copy(out=shared[t, h][:], in_=s_ps[:])

        for g in range(2):
            entries = slice(g * LIST_HALF, (g + 1) * LIST_HALF)
            half_list = offsets[:, g * LIST_HALF // 16 : (g + 1) * LIST_HALF // 16]
            for t in range(2):
                nc.vector.tensor_tensor(
                    pages[t][:].indirect(half_list), p_plain[g][:, t, :], ga_rows[:, entries], MULT
                )
        for t in range(2, PACK):
            nc.vector.tensor_copy(pages[t][:].indirect(offsets[:]), pw[:, t - 2, :])

        y = [[held("y%d_%d" % (u, h), [P, 2, BANK], F32) for h in range(2)] for u in range(2)]
        out_rows = out_0.rearrange("(p t) c -> p t c", t=PACK)

        def add_page(engine, t, h):
            cols = slice(h * BANK, (h + 1) * BANK)
            row = y[t // 2][h][:, t % 2, :]
            engine.tensor_tensor(out=row, in0=shared[t, h][:], in1=pages[t][:, cols], op=ADD)
            nc.sync.dma_start(out=out_rows[:, t, cols], in_=row)

        y_bf = [
            held("y_bf%d" % h, [P, BANK, 2, 2], BF16, tag=tag) for h, tag in enumerate(("ws_dealt", "ws_scale_dealt"))
        ]

        def round_pair(copy, u, h):
            copy(out=y_bf[h][:, :, u, :], in_=y[u][h][:].rearrange("p e c -> p c e"))

        for h in range(2):
            for t in range(2):
                add_page(nc.gpsimd, t, h)
            round_pair(nc.scalar.copy, 0, h)
        for h in range(2):
            add_page(nc.gpsimd, 2, h)
        for h in range(2):
            add_page(nc.vector, PACK - 1, h)
        round_pair(nc.scalar.copy, 1, 0)
        round_pair(nc.vector.tensor_copy, 1, 1)

        y_scale = held("y_scale", [P, T], U8)
        out_words = out_1[0].rearrange("p c r -> p (c r)").bitcast(I32)
        for h in (1, 0):
            cols = slice(h * BANK, (h + 1) * BANK)
            y_codes = held("y_codes%d" % h, [P, BANK], U32)
            nc.vector.quantize_mx(
                out=y_codes[:].bitcast(FP8X4), scales=y_scale[:, cols],
                in_=y_bf[h][:].rearrange("p c u e -> p (c u e)"),
            )
            nc.sync.dma_start(out=out_words[:, cols], in_=y_codes[:].bitcast(I32))
        for quad in range(4):
            queue = nc.sync if quad % 2 else nc.scalar
            queue.dma_start(
                out=out_2[0, 4 * quad : 4 * quad + 4, :].bitcast(I32),
                in_=y_scale[32 * quad : 32 * quad + 4, :].bitcast(I32),
            )
